import numpy as np
import ml_dtypes


def mxq(x, axis, fmt="e4m3"):
    dtype, down = {"e4m3": (ml_dtypes.float8_e4m3fn, 7), "e5m2": (ml_dtypes.float8_e5m2, 14)}[fmt]
    v = np.moveaxis(np.asarray(x, np.float32).astype(ml_dtypes.bfloat16).astype(np.float64), axis, -1)
    blocks = v.reshape(v.shape[:-1] + (-1, 32))
    amax = np.abs(blocks).max(-1, keepdims=True)
    byte = np.maximum(np.where(amax > 0, np.frexp(amax)[1] - 1 + 127, 0) - down, 1)
    scale = np.exp2(byte - 127.0)
    codes = (blocks / scale).astype(np.float32).astype(dtype).astype(np.float64)
    return np.moveaxis((codes * scale).reshape(v.shape), -1, axis)


WIDE = False


def mx_kscale(k):
    if not WIDE:
        return np.ones(k)
    levels = np.array([18, -18])
    if k % 512:
        return np.exp2(np.random.permutation(np.resize(levels, k // 32))).repeat(32)
    a = np.empty((k // 512, 16))
    for p in range(k // 512):
        a[p, :8] = np.random.permutation(np.resize(levels, 8))
        for g in range(8):
            far = levels[np.abs(levels - a[p, g]) >= 10]
            a[p, g + 8] = far[np.random.randint(len(far))]
    return np.exp2(a.ravel()).repeat(32)


def f64(x):
    return np.asarray(x).astype(np.float64)


def striped(idx):
    return np.tile(np.asarray(idx).reshape(-1, 16).T, (8, 1)).astype(np.uint16)


def unstriped(offs):
    return offs[:16].T.reshape(-1).astype(np.int64)

def planes(y):
    n, m = y.shape
    v = y.astype(np.float32).astype(ml_dtypes.bfloat16).astype(np.float64).reshape(n // 32, 32, m)
    top = np.abs(v).max(1)
    byte = np.clip(np.where(top > 0, np.frexp(top)[1] - 1 + 127 - 7, 1), 1, 254)
    codes = (v * np.exp2(127.0 - byte)[:, None, :]).reshape(n, m).astype(np.float32).astype(ml_dtypes.float8_e4m3fn).view(np.uint8)
    words = codes.reshape(n // 512, 128, 4, m).transpose(0, 1, 3, 2)
    return np.ascontiguousarray(words), np.ascontiguousarray(byte.astype(np.uint8).reshape(n // 512, 16, m))


def setup_inputs():
    n = np.random.standard_normal
    uni = np.random.uniform
    idx = np.random.permutation(2048)[:512]
    w_ = uni(0.2, 1.5, (512, 2048))
    f_l = mx_kscale(512)
    f_r = mx_kscale(512)
    return {
        "fT": (uni(0.2, 1.5, (512, 512)) * f_r[None, :]).astype(np.float32),
        "vT": (uni(0.1, 2.0, (512, 2048)) / f_r[:, None]).astype(np.float32),
        "H": (uni(0.5, 1.5, (512, 512)) * f_l[None, :]).astype(np.float32),
        "wT": (w_ / f_l[:, None]).astype(np.float32),
        "wU": (w_).astype(np.float32),
        "fk": (uni(0.5, 1.5, (512, 1))).astype(np.float32),
        "offs": striped(idx),
    }


def reference(fT, vT, H, wT, wU, fk, offs):
    idx = unstriped(offs)
    vT_i = f64(vT)[:, idx]
    w = f64(wT)[:, idx]
    v = f64(wU)[:, idx]
    num = mxq(f64(fT), 1, "e4m3") @ mxq(vT_i, 0, "e4m3")
    den = mxq(f64(H), 1, "e4m3") @ mxq(w, 0, "e4m3")
    nw = v * f64(fk) * num / (den + 0.001)
    out_0 = np.zeros((512, 2048))
    out_0[:, idx] = nw
    return (out_0,) + planes(out_0)

@@ -1,0 +1,197 @@
+from contextlib import ExitStack
+
+import concourse.mybir as mybir
+from concourse.masks import make_identity
+
+K, R, T, SLOTS = 512, 512, 2048, 512
+FLOPS = 2 * 2 * K * R * SLOTS
+EPS = 0.001
+
+F32 = mybir.dt.float32
+BF16 = mybir.dt.bfloat16
+I32 = mybir.dt.int32
+U32 = mybir.dt.uint32
+U16 = mybir.dt.uint16
+U8 = mybir.dt.uint8
+FP8X4 = mybir.dt.float8_e4m3fn_x4
+ACT = mybir.ActivationFunctionType
+MULT = mybir.AluOpType.mult
+
+P = 128
+LANES = 4
+CHUNKS = (128, 128, 256, 512, 512, 256, 256)
+SCALAR_WEAVES = 2
+STORE_AFTER = (2, 3, 4, 5, 6)
+
+
+def tile_attend_gnmf_pl_kernel(tc, fT, vT, H, wT, wU, fk, offs, out_0, out_1, out_2):
+    nc = tc.nc
+    with ExitStack() as ctx:
+        keep = ctx.enter_context(tc.tile_pool(name="keep", bufs=1))
+        ring = ctx.enter_context(tc.tile_pool(name="ring", bufs=2))
+        psum = ctx.enter_context(tc.psum_pool(name="psum", bufs=1))
+
+        def by_lane(table):
+            return table.rearrange("(p t) c -> p t c", t=LANES)
+
+        def load_lane(name, table, t):
+            plane = keep.tile([P, T], F32, name=f"{name}{t}", tag=f"{name}{t}", align_bytes=64)
+            nc.sync.dma_start(plane[:], by_lane(table)[:, t, :])
+            return plane
+
+        h_raw = keep.tile([P, LANES, R], F32, name="h_raw")
+        nc.sync.dma_start(h_raw[:], by_lane(H))
+        offsets = keep.tile([P, SLOTS // 16], U16, name="offsets")
+        nc.sync.dma_start(offsets[:], offs)
+        fk_sb = keep.tile([P, LANES], F32, name="fk_sb")
+        nc.sync.dma_start(fk_sb[:], fk.rearrange("(p t) o -> p (t o)", t=LANES))
+        w_raw = [load_lane("w_raw", wT, t) for t in range(LANES)]
+        v_raw = [load_lane("v_raw", vT, t) for t in range(LANES)]
+        f_first = keep.tile([P, R], F32, name="f_first")
+        nc.sync.dma_start(f_first[:], by_lane(fT)[:, 0, :])
+        f_rest = keep.tile([P, LANES - 1, R], F32, name="f_rest")
+        nc.sync.dma_start(f_rest[:], by_lane(fT)[:, 1:, :])
+        u_raw = [load_lane("u_raw", wU, t) for t in range(LANES)]
+
+        identity = keep.tile([P, P], F32, name="identity")
+        make_identity(nc, identity[:])
+
+        warm_in = keep.tile([P, 1], F32, name="warm_in")
+        nc.vector.memset(warm_in[:], 1.0)
+        warm_out = keep.tile([P, 1], F32, name="warm_out")
+        nc.scalar.activation(warm_out[:], warm_in[:], ACT.Abs_reciprocal_sqrt)
+
+        result = [keep.tile([P, T], F32, name=f"result{t}") for t in range(LANES)]
+        for t in range(LANES):
+            nc.vector.memset(result[t][:], 0.0)
+
+        def turn(rows, woven):
+            bank = psum.tile([P, LANES, P], F32, name="bank", tag="turn", bufs=3)
+            for j in range(LANES):
+                nc.tensor.transpose(bank[:, j, :], rows[:, j:R:LANES], identity[:])
+            nc.scalar.copy(woven, bank[:].rearrange("p j m -> p m j"))
+
+        def quantize(codes, scales, woven):
+            nc.vector.quantize_mx(out=codes.bitcast(FP8X4), scales=scales, in_=woven.rearrange("p c j -> p (c j)"))
+
+        def gather_and_quantize(name, raw, tags):
+            woven = keep.tile([P, SLOTS, LANES], BF16, name=f"{name}_woven", tag=f"{name}_woven", align_bytes=64)
+            for t in range(LANES):
+                nc.vector.tensor_copy(woven[:, :, t], raw[t][:].indirect(offsets[:]))
+            codes = keep.tile([P, SLOTS], U32, name=f"{name}_codes", tag=tags[0], align_bytes=64)
+            scales = keep.tile([P, SLOTS], U8, name=f"{name}_scales", tag=tags[1], align_bytes=64)
+            quantize(codes[:], scales[:], woven[:])
+            return codes, scales
+
+        def product(tag, bufs, left, right):
+            bank = psum.tile([P, SLOTS], F32, name=tag, tag=tag, bufs=bufs)
+            nc.tensor.matmul_mx(
+                out=bank[:],
+                lhsT=left[0].bitcast(FP8X4),
+                lhsT_scale=left[1],
+                rhs=right[0][:].bitcast(FP8X4),
+                rhs_scale=right[1][:],
+                start=True,
+                stop=True,
+            )
+            return bank
+
+        h_woven = keep.tile([P, K, LANES], BF16, name="h_woven", tag="h_woven", align_bytes=64)
+        for t in range(LANES):
+            turn(h_raw[:, t, :], h_woven[:, t * P : (t + 1) * P, :])
+        h_codes = keep.tile([P, K], U32, name="h_codes", align_bytes=64)
+        h_scales = keep.tile([P, K], U8, name="h_scales", align_bytes=64)
+        quantize(h_codes[:], h_scales[:], h_woven[:])
+        w_mx = gather_and_quantize("w", w_raw, ("w_codes", "w_scales"))
+        parts = []
+        for t in range(LANES):
+            den = product("den", 3, (h_codes[:, t * P : (t + 1) * P], h_scales[:, t * P : (t + 1) * P]), w_mx)
+            root = ring.tile([P, SLOTS], F32, name="root")
+            nc.scalar.activation(root[:], den[:], ACT.Abs_reciprocal_sqrt, bias=EPS)
+            sign = keep.tile([P, SLOTS], F32, name=f"sign{t}")
+            nc.scalar.activation(sign[:], den[:], ACT.Sign, bias=EPS)
+            size = keep.tile([P, SLOTS], F32, name=f"size{t}")
+            nc.scalar.activation(size[:], root[:], ACT.Square)
+            parts.append((size, sign))
+
+        def prepare_f(t, rows):
+            woven = keep.tile([P, P, LANES], BF16, name=f"f_woven{t}", tag=f"f_woven{t}", align_bytes=64)
+            turn(rows, woven[:])
+            codes = keep.tile([P, P], U32, name=f"f_codes{t}", tag=("f_codes0", "u_raw0", "v_raw1", "ratio0")[t], align_bytes=64)
+            scales = keep.tile([P, P], U8, name=f"f_scales{t}", align_bytes=64)
+            quantize(codes[:], scales[:], woven[:])
+            return codes[:], scales[:]
+
+        v_mx = gather_and_quantize("v", v_raw, ("v_codes", "v_scales"))
+
+        inverse = []
+        for t, tag in enumerate(("v_raw1", "v_raw2", "v_raw3", "v_woven")):
+            inv = keep.tile([P, SLOTS], F32, name=f"inv{t}", tag=tag, align_bytes=64)
+            nc.vector.tensor_tensor(inv[:], parts[t][0][:], parts[t][1][:], MULT)
+            inverse.append(inv)
+
+        def numerator(t, rows):
+            num = product("num", 2, prepare_f(t, rows), v_mx)
+            scaled = keep.tile([P, SLOTS], F32, name=f"scaled{t}")
+            nc.scalar.activation(scaled[:], num[:], ACT.Copy, scale=fk_sb[:, t : t + 1])
+            return scaled
+
+        def update(t, scaled):
+            ratio = keep.tile([P, SLOTS], F32, name=f"ratio{t}", tag=f"ratio{t}", align_bytes=64)
+            nc.vector.tensor_tensor(ratio[:], u_raw[t][:].indirect(offsets[:]), inverse[t][:], MULT)
+            nc.vector.tensor_tensor(result[t][:].indirect(offsets[:]), ratio[:], scaled[:], MULT)
+            nc.sync.dma_start(by_lane(out_0)[:, t, :], result[t][:])
+
+        numerators = [numerator(0, f_first[:])]
+        update(0, numerators[0])
+        numerators.extend(numerator(t, f_rest[:, t - 1, :]) for t in range(1, LANES))
+        for t in range(1, LANES):
+            update(t, numerators[t])
+
+        starts = [sum(CHUNKS[:c]) for c in range(len(CHUNKS))]
+        pairs = [
+            keep.tile([P, 2, width, 2], BF16, name=f"pairs{c}", align_bytes=64)
+            for c, width in enumerate(CHUNKS)
+        ]
+        for t in range(LANES):
+            for c, width in enumerate(CHUNKS):
+                nc.scalar.copy(pairs[c][:, t // 2, :, t % 2], result[t][:, starts[c] : starts[c] + width])
+
+        y_scales = keep.tile([P, T], U8, name="y_scales", align_bytes=64)
+        words_out = out_1.rearrange("a p c l -> p (a c l)").bitcast(I32)
+        runs = []
+        for c in STORE_AFTER:
+            first = runs[-1][1] if runs else 0
+            end = starts[c] + CHUNKS[c]
+            runs.append((first, end, keep.tile([P, end - first], U32, name=f"y_codes{c}", align_bytes=64)))
+        woven = []
+
+        def weave(c):
+            width = CHUNKS[c]
+            tile = keep.tile([P, width, LANES], BF16, name=f"y_woven{c}", tag=("w_raw0", "w_raw1", "w_raw2", "w_raw3", "v_raw0", "u_raw1", "u_raw2")[c], align_bytes=64)
+            last = c >= len(CHUNKS) - SCALAR_WEAVES
+            word = U32 if last else I32
+            src = pairs[c][:].rearrange("p h c e -> p (h c e)").bitcast(word).rearrange("p (h c) -> p c h", h=2)
+            dst = tile[:].rearrange("p c j -> p (c j)").bitcast(word).rearrange("p (c h) -> p c h", h=2)
+            if last:
+                nc.scalar.copy(dst, src)
+            else:
+                nc.vector.tensor_copy(dst, src)
+            woven.append(tile)
+
+        def finish(c):
+            cols = slice(starts[c], starts[c] + CHUNKS[c])
+            first, end, codes = [run for run in runs if run[1] >= cols.stop][0]
+            quantize(codes[:, cols.start - first : cols.stop - first], y_scales[:, cols], woven[c][:])
+            if cols.stop == end:
+                nc.sync.dma_start(words_out[:, first:end], codes[:].bitcast(I32))
+
+        weave(0)
+        for c in range(1, len(CHUNKS)):
+            weave(c)
+            finish(c - 1)
+        finish(len(CHUNKS) - 1)
+
+        scales_out = out_2.rearrange("a b c -> (a b) c").bitcast(I32)
+        for q in range(4):
+            nc.scalar.dma_start(scales_out[4 * q : 4 * q + 4, :], y_scales[32 * q : 32 * q + 4, :].bitcast(I32))

@@ -19,9 +19,9 @@ MULT = mybir.AluOpType.mult
 
 P = 128
 LANES = 4
-CHUNKS = (128, 128, 256, 512, 512, 256, 256)
+CHUNKS = (256, 256, 512, 512, 256, 256)
 SCALAR_WEAVES = 2
-STORE_AFTER = (2, 3, 4, 5, 6)
+STORE_AFTER = (2, 4, 5)
 
 
 def tile_attend_gnmf_pl_kernel(tc, fT, vT, H, wT, wU, fk, offs, out_0, out_1, out_2):
@@ -49,11 +49,12 @@ def tile_attend_gnmf_pl_kernel(tc, fT, vT, H, wT, wU, fk, offs, out_0, out_1, ou
         v_raw = [load_lane("v_raw", vT, t) for t in range(LANES)]
         f_first = keep.tile([P, R], F32, name="f_first")
         nc.sync.dma_start(f_first[:], by_lane(fT)[:, 0, :])
-        f_rest = keep.tile([P, LANES - 1, R], F32, name="f_rest")
+        u_raw = [load_lane("u_raw", wU, 0)]
+        f_rest = keep.tile([P, LANES - 1, R], F32, name="f_rest", tag="f_rest", align_bytes=64)
         nc.sync.dma_start(f_rest[:], by_lane(fT)[:, 1:, :])
-        u_raw = [load_lane("u_raw", wU, t) for t in range(LANES)]
+        u_raw.extend(load_lane("u_raw", wU, t) for t in range(1, LANES))
 
-        identity = keep.tile([P, P], F32, name="identity")
+        identity = keep.tile([P, P], F32, name="identity", tag="identity", align_bytes=64)
         make_identity(nc, identity[:])
 
         warm_in = keep.tile([P, 1], F32, name="warm_in")
@@ -65,11 +66,15 @@ def tile_attend_gnmf_pl_kernel(tc, fT, vT, H, wT, wU, fk, offs, out_0, out_1, ou
         for t in range(LANES):
             nc.vector.memset(result[t][:], 0.0)
 
-        def turn(rows, woven):
-            bank = psum.tile([P, LANES, P], F32, name="bank", tag="turn", bufs=3)
-            for j in range(LANES):
-                nc.tensor.transpose(bank[:, j, :], rows[:, j:R:LANES], identity[:])
-            nc.scalar.copy(woven, bank[:].rearrange("p j m -> p m j"))
+        def turn(name, rows, woven):
+            halves = keep.tile([P, 2, P, 2], BF16, name=name, tag=name, align_bytes=64)
+            nc.scalar.copy(halves[:], rows.rearrange("m (p h e) -> m h p e", h=2, e=2))
+            words = halves[:].rearrange("m h p e -> m (h p e)").bitcast(F32)
+            bank = psum.tile([P, 2, P], F32, name="bank", tag="turn", bufs=2)
+            for h in range(2):
+                nc.tensor.transpose(bank[:, h, :], words[:, h * P : (h + 1) * P], identity[:])
+            woven_words = woven.rearrange("p m j -> p (m j)").bitcast(F32).rearrange("p (m h) -> p m h", h=2)
+            nc.scalar.copy(woven_words, bank[:].rearrange("p h m -> p m h"))
 
         def quantize(codes, scales, woven):
             nc.vector.quantize_mx(out=codes.bitcast(FP8X4), scales=scales, in_=woven.rearrange("p c j -> p (c j)"))
@@ -98,7 +103,7 @@ def tile_attend_gnmf_pl_kernel(tc, fT, vT, H, wT, wU, fk, offs, out_0, out_1, ou
 
         h_woven = keep.tile([P, K, LANES], BF16, name="h_woven", tag="h_woven", align_bytes=64)
         for t in range(LANES):
-            turn(h_raw[:, t, :], h_woven[:, t * P : (t + 1) * P, :])
+            turn(f"h_halves{t}", h_raw[:, t, :], h_woven[:, t * P : (t + 1) * P, :])
         h_codes = keep.tile([P, K], U32, name="h_codes", align_bytes=64)
         h_scales = keep.tile([P, K], U8, name="h_scales", align_bytes=64)
         quantize(h_codes[:], h_scales[:], h_woven[:])
@@ -116,9 +121,9 @@ def tile_attend_gnmf_pl_kernel(tc, fT, vT, H, wT, wU, fk, offs, out_0, out_1, ou
 
         def prepare_f(t, rows):
             woven = keep.tile([P, P, LANES], BF16, name=f"f_woven{t}", tag=f"f_woven{t}", align_bytes=64)
-            turn(rows, woven[:])
-            codes = keep.tile([P, P], U32, name=f"f_codes{t}", tag=("f_codes0", "u_raw0", "v_raw1", "ratio0")[t], align_bytes=64)
-            scales = keep.tile([P, P], U8, name=f"f_scales{t}", align_bytes=64)
+            turn(f"f_halves{t}", rows, woven[:])
+            codes = keep.tile([P, P], U32, name=f"f_codes{t}", tag=f"f_codes{t}", align_bytes=64)
+            scales = keep.tile([P, P], U8, name=f"f_scales{t}", tag=f"f_scales{t}", align_bytes=64)
             quantize(codes[:], scales[:], woven[:])
             return codes[:], scales[:]
 
@@ -131,13 +136,13 @@ def tile_attend_gnmf_pl_kernel(tc, fT, vT, H, wT, wU, fk, offs, out_0, out_1, ou
             inverse.append(inv)
 
         def numerator(t, rows):
-            num = product("num", 2, prepare_f(t, rows), v_mx)
+            num = product("num", 3, prepare_f(t, rows), v_mx)
             scaled = keep.tile([P, SLOTS], F32, name=f"scaled{t}")
             nc.scalar.activation(scaled[:], num[:], ACT.Copy, scale=fk_sb[:, t : t + 1])
             return scaled
 
         def update(t, scaled):
-            ratio = keep.tile([P, SLOTS], F32, name=f"ratio{t}", tag=f"ratio{t}", align_bytes=64)
+            ratio = keep.tile([P, SLOTS], F32, name=f"ratio{t}", tag="f_woven3" if t == 1 else f"ratio{t}", align_bytes=64)
             nc.vector.tensor_tensor(ratio[:], u_raw[t][:].indirect(offsets[:]), inverse[t][:], MULT)
             nc.vector.tensor_tensor(result[t][:].indirect(offsets[:]), ratio[:], scaled[:], MULT)
             nc.sync.dma_start(by_lane(out_0)[:, t, :], result[t][:])
@@ -149,8 +154,9 @@ def tile_attend_gnmf_pl_kernel(tc, fT, vT, H, wT, wU, fk, offs, out_0, out_1, ou
             update(t, numerators[t])
 
         starts = [sum(CHUNKS[:c]) for c in range(len(CHUNKS))]
+        pair_tags = ("f_scales2", "v_codes", "f_codes2", "f_codes3", "v_scales", "f_scales3")
         pairs = [
-            keep.tile([P, 2, width, 2], BF16, name=f"pairs{c}", align_bytes=64)
+            keep.tile([P, 2, width, 2], BF16, name=f"pairs{c}", tag=pair_tags[c], align_bytes=64)
             for c, width in enumerate(CHUNKS)
         ]
         for t in range(LANES):
@@ -168,7 +174,7 @@ def tile_attend_gnmf_pl_kernel(tc, fT, vT, H, wT, wU, fk, offs, out_0, out_1, ou
 
         def weave(c):
             width = CHUNKS[c]
-            tile = keep.tile([P, width, LANES], BF16, name=f"y_woven{c}", tag=("w_raw0", "w_raw1", "w_raw2", "w_raw3", "v_raw0", "u_raw1", "u_raw2")[c], align_bytes=64)
+            tile = keep.tile([P, width, LANES], BF16, name=f"y_woven{c}", tag=("w_raw0", "w_raw1", "w_raw2", "w_raw3", "v_raw0", "u_raw1")[c], align_bytes=64)
             last = c >= len(CHUNKS) - SCALAR_WEAVES
             word = U32 if last else I32
             src = pairs[c][:].rearrange("p h c e -> p (h c e)").bitcast(word).rearrange("p (h c) -> p c h", h=2)

@@ -21,7 +21,7 @@ P = 128
 LANES = 4
 CHUNKS = (256, 256, 512, 512, 256, 256)
 SCALAR_WEAVES = 2
-STORE_AFTER = (2, 4, 5)
+STORE_AFTER = (2, 3, 4, 5)
 
 
 def tile_attend_gnmf_pl_kernel(tc, fT, vT, H, wT, wU, fk, offs, out_0, out_1, out_2):
@@ -108,16 +108,18 @@ def tile_attend_gnmf_pl_kernel(tc, fT, vT, H, wT, wU, fk, offs, out_0, out_1, ou
         h_scales = keep.tile([P, K], U8, name="h_scales", align_bytes=64)
         quantize(h_codes[:], h_scales[:], h_woven[:])
         w_mx = gather_and_quantize("w", w_raw, ("w_codes", "w_scales"))
-        parts = []
+        inverse = []
         for t in range(LANES):
             den = product("den", 3, (h_codes[:, t * P : (t + 1) * P], h_scales[:, t * P : (t + 1) * P]), w_mx)
             root = ring.tile([P, SLOTS], F32, name="root")
             nc.scalar.activation(root[:], den[:], ACT.Abs_reciprocal_sqrt, bias=EPS)
-            sign = keep.tile([P, SLOTS], F32, name=f"sign{t}")
+            sign = ring.tile([P, SLOTS], F32, name="sign")
             nc.scalar.activation(sign[:], den[:], ACT.Sign, bias=EPS)
-            size = keep.tile([P, SLOTS], F32, name=f"size{t}")
+            size = ring.tile([P, SLOTS], F32, name="size")
             nc.scalar.activation(size[:], root[:], ACT.Square)
-            parts.append((size, sign))
+            inv = keep.tile([P, SLOTS], F32, name=f"inv{t}")
+            nc.gpsimd.tensor_tensor(inv[:], size[:], sign[:], MULT)
+            inverse.append(inv)
 
         def prepare_f(t, rows):
             woven = keep.tile([P, P, LANES], BF16, name=f"f_woven{t}", tag=f"f_woven{t}", align_bytes=64)
@@ -128,12 +130,6 @@ def tile_attend_gnmf_pl_kernel(tc, fT, vT, H, wT, wU, fk, offs, out_0, out_1, ou
             return codes[:], scales[:]
 
         v_mx = gather_and_quantize("v", v_raw, ("v_codes", "v_scales"))
-
-        inverse = []
-        for t, tag in enumerate(("v_raw1", "v_raw2", "v_raw3", "v_woven")):
-            inv = keep.tile([P, SLOTS], F32, name=f"inv{t}", tag=tag, align_bytes=64)
-            nc.vector.tensor_tensor(inv[:], parts[t][0][:], parts[t][1][:], MULT)
-            inverse.append(inv)
 
         def numerator(t, rows):
             num = product("num", 3, prepare_f(t, rows), v_mx)

@@ -46,9 +46,9 @@ def tile_attend_gnmf_pl_kernel(tc, fT, vT, H, wT, wU, fk, offs, out_0, out_1, ou
         fk_sb = keep.tile([P, LANES], F32, name="fk_sb")
         nc.sync.dma_start(fk_sb[:], fk.rearrange("(p t) o -> p (t o)", t=LANES))
         w_raw = [load_lane("w_raw", wT, t) for t in range(LANES)]
-        v_raw = [load_lane("v_raw", vT, t) for t in range(LANES)]
         f_first = keep.tile([P, R], F32, name="f_first")
         nc.sync.dma_start(f_first[:], by_lane(fT)[:, 0, :])
+        v_raw = [load_lane("v_raw", vT, t) for t in range(LANES)]
         u_raw = [load_lane("u_raw", wU, 0)]
         f_rest = keep.tile([P, LANES - 1, R], F32, name="f_rest", tag="f_rest", align_bytes=64)
         nc.sync.dma_start(f_rest[:], by_lane(fT)[:, 1:, :])
@@ -108,6 +108,16 @@ def tile_attend_gnmf_pl_kernel(tc, fT, vT, H, wT, wU, fk, offs, out_0, out_1, ou
         h_scales = keep.tile([P, K], U8, name="h_scales", align_bytes=64)
         quantize(h_codes[:], h_scales[:], h_woven[:])
         w_mx = gather_and_quantize("w", w_raw, ("w_codes", "w_scales"))
+
+        def prepare_f(t, rows):
+            woven = keep.tile([P, P, LANES], BF16, name=f"f_woven{t}", tag=f"f_woven{t}", align_bytes=64)
+            turn(f"f_halves{t}", rows, woven[:])
+            codes = keep.tile([P, P], U32, name=f"f_codes{t}", tag=f"f_codes{t}", align_bytes=64)
+            scales = keep.tile([P, P], U8, name=f"f_scales{t}", tag=f"f_scales{t}", align_bytes=64)
+            quantize(codes[:], scales[:], woven[:])
+            return codes[:], scales[:]
+
+        f_first_mx = prepare_f(0, f_first[:])
         inverse = []
         for t in range(LANES):
             den = product("den", 3, (h_codes[:, t * P : (t + 1) * P], h_scales[:, t * P : (t + 1) * P]), w_mx)
@@ -121,18 +131,10 @@ def tile_attend_gnmf_pl_kernel(tc, fT, vT, H, wT, wU, fk, offs, out_0, out_1, ou
             nc.gpsimd.tensor_tensor(inv[:], size[:], sign[:], MULT)
             inverse.append(inv)
 
-        def prepare_f(t, rows):
-            woven = keep.tile([P, P, LANES], BF16, name=f"f_woven{t}", tag=f"f_woven{t}", align_bytes=64)
-            turn(f"f_halves{t}", rows, woven[:])
-            codes = keep.tile([P, P], U32, name=f"f_codes{t}", tag=f"f_codes{t}", align_bytes=64)
-            scales = keep.tile([P, P], U8, name=f"f_scales{t}", tag=f"f_scales{t}", align_bytes=64)
-            quantize(codes[:], scales[:], woven[:])
-            return codes[:], scales[:]
-
         v_mx = gather_and_quantize("v", v_raw, ("v_codes", "v_scales"))
 
-        def numerator(t, rows):
-            num = product("num", 3, prepare_f(t, rows), v_mx)
+        def numerator(t, f_mx):
+            num = product("num", 3, f_mx, v_mx)
             scaled = keep.tile([P, SLOTS], F32, name=f"scaled{t}")
             nc.scalar.activation(scaled[:], num[:], ACT.Copy, scale=fk_sb[:, t : t + 1])
             return scaled
@@ -143,9 +145,9 @@ def tile_attend_gnmf_pl_kernel(tc, fT, vT, H, wT, wU, fk, offs, out_0, out_1, ou
             nc.vector.tensor_tensor(result[t][:].indirect(offsets[:]), ratio[:], scaled[:], MULT)
             nc.sync.dma_start(by_lane(out_0)[:, t, :], result[t][:])
 
-        numerators = [numerator(0, f_first[:])]
+        numerators = [numerator(0, f_first_mx)]
         update(0, numerators[0])
-        numerators.extend(numerator(t, f_rest[:, t - 1, :]) for t in range(1, LANES))
+        numerators.extend(numerator(t, prepare_f(t, f_rest[:, t - 1, :])) for t in range(1, LANES))
         for t in range(1, LANES):
             update(t, numerators[t])
 

@@ -3,9 +3,9 @@ from contextlib import ExitStack
 import concourse.mybir as mybir
 from concourse.masks import make_identity
 
-K, R, T, SLOTS = 512, 512, 2048, 512
+K, R, ITEMS, SLOTS = 512, 512, 2048, 512
 FLOPS = 2 * 2 * K * R * SLOTS
-EPS = 0.001
+EPS_INVERSE_SQUARE = 1.0e6
 
 F32 = mybir.dt.float32
 BF16 = mybir.dt.bfloat16
@@ -19,9 +19,14 @@ MULT = mybir.AluOpType.mult
 
 P = 128
 LANES = 4
+QUADRANT = 32
+ALIGN = 64
+
 CHUNKS = (256, 256, 512, 512, 256, 256)
 SCALAR_WEAVES = 2
 STORE_AFTER = (2, 3, 4, 5)
+
+TURN_BANKS, DEN_BANKS, NUM_BANKS = 2, 3, 3
 
 
 def tile_attend_gnmf_pl_kernel(tc, fT, vT, H, wT, wU, fk, offs, out_0, out_1, out_2):
@@ -31,171 +36,173 @@ def tile_attend_gnmf_pl_kernel(tc, fT, vT, H, wT, wU, fk, offs, out_0, out_1, ou
         ring = ctx.enter_context(tc.tile_pool(name="ring", bufs=2))
         psum = ctx.enter_context(tc.psum_pool(name="psum", bufs=1))
 
-        def by_lane(table):
-            return table.rearrange("(p t) c -> p t c", t=LANES)
+        def slot(shape, dtype, name, after=None):
+            return keep.tile(shape, dtype, name=name, tag=after or name, align_bytes=ALIGN)
+
+        def by_lane(rows):
+            return rows.rearrange("(p t) c -> p t c", t=LANES)
 
         def load_lane(name, table, t):
-            plane = keep.tile([P, T], F32, name=f"{name}{t}", tag=f"{name}{t}", align_bytes=64)
-            nc.sync.dma_start(plane[:], by_lane(table)[:, t, :])
-            return plane
+            tile = slot([P, ITEMS], F32, f"{name}{t}")
+            nc.sync.dma_start(tile[:], by_lane(table)[:, t, :])
+            return tile
 
-        h_raw = keep.tile([P, LANES, R], F32, name="h_raw")
-        nc.sync.dma_start(h_raw[:], by_lane(H))
+        h_rows = keep.tile([P, LANES, R], F32, name="h_rows")
+        nc.sync.dma_start(h_rows[:], by_lane(H))
         offsets = keep.tile([P, SLOTS // 16], U16, name="offsets")
         nc.sync.dma_start(offsets[:], offs)
-        fk_sb = keep.tile([P, LANES], F32, name="fk_sb")
-        nc.sync.dma_start(fk_sb[:], fk.rearrange("(p t) o -> p (t o)", t=LANES))
-        w_raw = [load_lane("w_raw", wT, t) for t in range(LANES)]
+        fk_lanes = keep.tile([P, LANES], F32, name="fk_lanes")
+        nc.sync.dma_start(fk_lanes[:], fk.rearrange("(p t) o -> p (t o)", t=LANES))
+        w_table = [load_lane("w_table", wT, t) for t in range(LANES)]
         f_first = keep.tile([P, R], F32, name="f_first")
         nc.sync.dma_start(f_first[:], by_lane(fT)[:, 0, :])
-        v_raw = [load_lane("v_raw", vT, t) for t in range(LANES)]
-        u_raw = [load_lane("u_raw", wU, 0)]
-        f_rest = keep.tile([P, LANES - 1, R], F32, name="f_rest", tag="f_rest", align_bytes=64)
+        v_table = [load_lane("v_table", vT, t) for t in range(LANES)]
+        u_table = [load_lane("u_table", wU, 0)]
+        f_rest = keep.tile([P, LANES - 1, R], F32, name="f_rest")
         nc.sync.dma_start(f_rest[:], by_lane(fT)[:, 1:, :])
-        u_raw.extend(load_lane("u_raw", wU, t) for t in range(1, LANES))
+        u_table.extend(load_lane("u_table", wU, t) for t in range(1, LANES))
 
-        identity = keep.tile([P, P], F32, name="identity", tag="identity", align_bytes=64)
+        identity = keep.tile([P, P], F32, name="identity")
         make_identity(nc, identity[:])
 
-        warm_in = keep.tile([P, 1], F32, name="warm_in")
-        nc.vector.memset(warm_in[:], 1.0)
-        warm_out = keep.tile([P, 1], F32, name="warm_out")
-        nc.scalar.activation(warm_out[:], warm_in[:], ACT.Abs_reciprocal_sqrt)
+        eps_source = keep.tile([P, 1], F32, name="eps_source")
+        nc.vector.memset(eps_source[:], EPS_INVERSE_SQUARE)
+        eps = keep.tile([P, 1], F32, name="eps")
+        nc.scalar.activation(eps[:], eps_source[:], ACT.Abs_reciprocal_sqrt)
 
-        result = [keep.tile([P, T], F32, name=f"result{t}") for t in range(LANES)]
+        result = [keep.tile([P, ITEMS], F32, name=f"result{t}") for t in range(LANES)]
         for t in range(LANES):
             nc.vector.memset(result[t][:], 0.0)
 
         def turn(name, rows, woven):
-            halves = keep.tile([P, 2, P, 2], BF16, name=name, tag=name, align_bytes=64)
+            halves = keep.tile([P, 2, P, 2], BF16, name=name, align_bytes=ALIGN)
             nc.scalar.copy(halves[:], rows.rearrange("m (p h e) -> m h p e", h=2, e=2))
             words = halves[:].rearrange("m h p e -> m (h p e)").bitcast(F32)
-            bank = psum.tile([P, 2, P], F32, name="bank", tag="turn", bufs=2)
+            bank = psum.tile([P, 2, P], F32, name="turned", bufs=TURN_BANKS)
             for h in range(2):
                 nc.tensor.transpose(bank[:, h, :], words[:, h * P : (h + 1) * P], identity[:])
-            woven_words = woven.rearrange("p m j -> p (m j)").bitcast(F32).rearrange("p (m h) -> p m h", h=2)
+            woven_words = woven.rearrange("p m t -> p (m t)").bitcast(F32).rearrange("p (m h) -> p m h", h=2)
             nc.scalar.copy(woven_words, bank[:].rearrange("p h m -> p m h"))
 
         def quantize(codes, scales, woven):
-            nc.vector.quantize_mx(out=codes.bitcast(FP8X4), scales=scales, in_=woven.rearrange("p c j -> p (c j)"))
+            nc.vector.quantize_mx(out=codes.bitcast(FP8X4), scales=scales, in_=woven.rearrange("p c t -> p (c t)"))
 
-        def gather_and_quantize(name, raw, tags):
-            woven = keep.tile([P, SLOTS, LANES], BF16, name=f"{name}_woven", tag=f"{name}_woven", align_bytes=64)
+        def gather_and_quantize(name, table):
+            woven = slot([P, SLOTS, LANES], BF16, f"{name}_woven")
             for t in range(LANES):
-                nc.vector.tensor_copy(woven[:, :, t], raw[t][:].indirect(offsets[:]))
-            codes = keep.tile([P, SLOTS], U32, name=f"{name}_codes", tag=tags[0], align_bytes=64)
-            scales = keep.tile([P, SLOTS], U8, name=f"{name}_scales", tag=tags[1], align_bytes=64)
+                nc.vector.tensor_copy(woven[:, :, t], table[t][:].indirect(offsets[:]))
+            codes = slot([P, SLOTS], U32, f"{name}_codes")
+            scales = slot([P, SLOTS], U8, f"{name}_scales")
             quantize(codes[:], scales[:], woven[:])
-            return codes, scales
+            return codes[:], scales[:]
 
-        def product(tag, bufs, left, right):
-            bank = psum.tile([P, SLOTS], F32, name=tag, tag=tag, bufs=bufs)
+        def quantize_f(t, rows):
+            woven = slot([P, P, LANES], BF16, f"f_woven{t}")
+            turn(f"f_halves{t}", rows, woven[:])
+            codes = slot([P, P], U32, f"f_codes{t}")
+            scales = slot([P, P], U8, f"f_scales{t}")
+            quantize(codes[:], scales[:], woven[:])
+            return codes[:], scales[:]
+
+        def product(name, banks, stationary, moving):
+            bank = psum.tile([P, SLOTS], F32, name=name, bufs=banks)
             nc.tensor.matmul_mx(
                 out=bank[:],
-                lhsT=left[0].bitcast(FP8X4),
-                lhsT_scale=left[1],
-                rhs=right[0][:].bitcast(FP8X4),
-                rhs_scale=right[1][:],
+                lhsT=stationary[0].bitcast(FP8X4),
+                lhsT_scale=stationary[1],
+                rhs=moving[0].bitcast(FP8X4),
+                rhs_scale=moving[1],
                 start=True,
                 stop=True,
             )
             return bank
 
-        h_woven = keep.tile([P, K, LANES], BF16, name="h_woven", tag="h_woven", align_bytes=64)
+        h_woven = slot([P, K, LANES], BF16, "h_woven")
         for t in range(LANES):
-            turn(f"h_halves{t}", h_raw[:, t, :], h_woven[:, t * P : (t + 1) * P, :])
-        h_codes = keep.tile([P, K], U32, name="h_codes", align_bytes=64)
-        h_scales = keep.tile([P, K], U8, name="h_scales", align_bytes=64)
+            turn(f"h_halves{t}", h_rows[:, t, :], h_woven[:, t * P : (t + 1) * P, :])
+        h_codes = slot([P, K], U32, "h_codes")
+        h_scales = slot([P, K], U8, "h_scales")
         quantize(h_codes[:], h_scales[:], h_woven[:])
-        w_mx = gather_and_quantize("w", w_raw, ("w_codes", "w_scales"))
+        w_mx = gather_and_quantize("w", w_table)
+        f_first_mx = quantize_f(0, f_first[:])
 
-        def prepare_f(t, rows):
-            woven = keep.tile([P, P, LANES], BF16, name=f"f_woven{t}", tag=f"f_woven{t}", align_bytes=64)
-            turn(f"f_halves{t}", rows, woven[:])
-            codes = keep.tile([P, P], U32, name=f"f_codes{t}", tag=f"f_codes{t}", align_bytes=64)
-            scales = keep.tile([P, P], U8, name=f"f_scales{t}", tag=f"f_scales{t}", align_bytes=64)
-            quantize(codes[:], scales[:], woven[:])
-            return codes[:], scales[:]
-
-        f_first_mx = prepare_f(0, f_first[:])
         inverse = []
         for t in range(LANES):
-            den = product("den", 3, (h_codes[:, t * P : (t + 1) * P], h_scales[:, t * P : (t + 1) * P]), w_mx)
+            rows = slice(t * P, (t + 1) * P)
+            den = product("den", DEN_BANKS, (h_codes[:, rows], h_scales[:, rows]), w_mx)
             root = ring.tile([P, SLOTS], F32, name="root")
-            nc.scalar.activation(root[:], den[:], ACT.Abs_reciprocal_sqrt, bias=EPS)
+            nc.scalar.activation(root[:], den[:], ACT.Abs_reciprocal_sqrt, bias=eps[:])
             sign = ring.tile([P, SLOTS], F32, name="sign")
-            nc.scalar.activation(sign[:], den[:], ACT.Sign, bias=EPS)
+            nc.scalar.activation(sign[:], den[:], ACT.Sign, bias=eps[:])
             size = ring.tile([P, SLOTS], F32, name="size")
             nc.scalar.activation(size[:], root[:], ACT.Square)
-            inv = keep.tile([P, SLOTS], F32, name=f"inv{t}")
-            nc.gpsimd.tensor_tensor(inv[:], size[:], sign[:], MULT)
-            inverse.append(inv)
+            signed = keep.tile([P, SLOTS], F32, name=f"inverse{t}")
+            nc.gpsimd.tensor_tensor(signed[:], size[:], sign[:], MULT)
+            inverse.append(signed)
 
-        v_mx = gather_and_quantize("v", v_raw, ("v_codes", "v_scales"))
+        v_mx = gather_and_quantize("v", v_table)
 
         def numerator(t, f_mx):
-            num = product("num", 3, f_mx, v_mx)
+            num = product("num", NUM_BANKS, f_mx, v_mx)
             scaled = keep.tile([P, SLOTS], F32, name=f"scaled{t}")
-            nc.scalar.activation(scaled[:], num[:], ACT.Copy, scale=fk_sb[:, t : t + 1])
+            nc.scalar.activation(scaled[:], num[:], ACT.Copy, scale=fk_lanes[:, t : t + 1])
             return scaled
 
-        def update(t, scaled):
-            ratio = keep.tile([P, SLOTS], F32, name=f"ratio{t}", tag="f_woven3" if t == 1 else f"ratio{t}", align_bytes=64)
-            nc.vector.tensor_tensor(ratio[:], u_raw[t][:].indirect(offsets[:]), inverse[t][:], MULT)
+        def update(t, scaled, after=None):
+            ratio = slot([P, SLOTS], F32, f"ratio{t}", after)
+            nc.vector.tensor_tensor(ratio[:], u_table[t][:].indirect(offsets[:]), inverse[t][:], MULT)
             nc.vector.tensor_tensor(result[t][:].indirect(offsets[:]), ratio[:], scaled[:], MULT)
             nc.sync.dma_start(by_lane(out_0)[:, t, :], result[t][:])
 
-        numerators = [numerator(0, f_first_mx)]
-        update(0, numerators[0])
-        numerators.extend(numerator(t, prepare_f(t, f_rest[:, t - 1, :])) for t in range(1, LANES))
-        for t in range(1, LANES):
-            update(t, numerators[t])
+        update(0, numerator(0, f_first_mx))
+        later = [numerator(t, quantize_f(t, f_rest[:, t - 1, :])) for t in range(1, LANES)]
+        update(1, later[0], after=f"f_woven{LANES - 1}")
+        for t in range(2, LANES):
+            update(t, later[t - 1])
 
         starts = [sum(CHUNKS[:c]) for c in range(len(CHUNKS))]
-        pair_tags = ("f_scales2", "v_codes", "f_codes2", "f_codes3", "v_scales", "f_scales3")
-        pairs = [
-            keep.tile([P, 2, width, 2], BF16, name=f"pairs{c}", tag=pair_tags[c], align_bytes=64)
-            for c, width in enumerate(CHUNKS)
-        ]
+        pairs_after = ("f_scales2", "v_codes", "f_codes2", "f_codes3", "v_scales", "f_scales3")
+        pairs = [slot([P, 2, width, 2], BF16, f"pairs{c}", pairs_after[c]) for c, width in enumerate(CHUNKS)]
         for t in range(LANES):
             for c, width in enumerate(CHUNKS):
                 nc.scalar.copy(pairs[c][:, t // 2, :, t % 2], result[t][:, starts[c] : starts[c] + width])
 
-        y_scales = keep.tile([P, T], U8, name="y_scales", align_bytes=64)
-        words_out = out_1.rearrange("a p c l -> p (a c l)").bitcast(I32)
-        runs = []
+        y_scales = slot([P, ITEMS], U8, "y_scales")
+        words_out = out_1.rearrange("a p c t -> p (a c t)").bitcast(I32)
+        stores = []
         for c in STORE_AFTER:
-            first = runs[-1][1] if runs else 0
+            first = stores[-1][1] if stores else 0
             end = starts[c] + CHUNKS[c]
-            runs.append((first, end, keep.tile([P, end - first], U32, name=f"y_codes{c}", align_bytes=64)))
-        woven = []
+            stores.append((first, end, slot([P, end - first], U32, f"y_codes{c}")))
+
+        woven_after = ("w_table0", "w_table1", "w_table2", "w_table3", "v_table0", "u_table1")
 
         def weave(c):
-            width = CHUNKS[c]
-            tile = keep.tile([P, width, LANES], BF16, name=f"y_woven{c}", tag=("w_raw0", "w_raw1", "w_raw2", "w_raw3", "v_raw0", "u_raw1")[c], align_bytes=64)
-            last = c >= len(CHUNKS) - SCALAR_WEAVES
-            word = U32 if last else I32
+            woven = slot([P, CHUNKS[c], LANES], BF16, f"y_woven{c}", woven_after[c])
+            on_scalar = c >= len(CHUNKS) - SCALAR_WEAVES
+            word = U32 if on_scalar else I32
             src = pairs[c][:].rearrange("p h c e -> p (h c e)").bitcast(word).rearrange("p (h c) -> p c h", h=2)
-            dst = tile[:].rearrange("p c j -> p (c j)").bitcast(word).rearrange("p (c h) -> p c h", h=2)
-            if last:
+            dst = woven[:].rearrange("p c t -> p (c t)").bitcast(word).rearrange("p (c h) -> p c h", h=2)
+            if on_scalar:
                 nc.scalar.copy(dst, src)
             else:
                 nc.vector.tensor_copy(dst, src)
-            woven.append(tile)
+            return woven
 
-        def finish(c):
-            cols = slice(starts[c], starts[c] + CHUNKS[c])
-            first, end, codes = [run for run in runs if run[1] >= cols.stop][0]
-            quantize(codes[:, cols.start - first : cols.stop - first], y_scales[:, cols], woven[c][:])
-            if cols.stop == end:
+        def quantize_chunk(c, woven):
+            start, stop = starts[c], starts[c] + CHUNKS[c]
+            first, end, codes = [store for store in stores if store[1] >= stop][0]
+            quantize(codes[:, start - first : stop - first], y_scales[:, start:stop], woven[:])
+            if stop == end:
                 nc.sync.dma_start(words_out[:, first:end], codes[:].bitcast(I32))
 
-        weave(0)
+        y_woven = [weave(0)]
         for c in range(1, len(CHUNKS)):
-            weave(c)
-            finish(c - 1)
-        finish(len(CHUNKS) - 1)
+            y_woven.append(weave(c))
+            quantize_chunk(c - 1, y_woven[c - 1])
+        quantize_chunk(len(CHUNKS) - 1, y_woven[-1])
 
         scales_out = out_2.rearrange("a b c -> (a b) c").bitcast(I32)
-        for q in range(4):
-            nc.scalar.dma_start(scales_out[4 * q : 4 * q + 4, :], y_scales[32 * q : 32 * q + 4, :].bitcast(I32))
+        for q in range(P // QUADRANT):
+            queue = nc.scalar if q < 2 else nc.sync
+            queue.dma_start(scales_out[4 * q : 4 * q + 4, :], y_scales[QUADRANT * q : QUADRANT * q + 4, :].bitcast(I32))

from contextlib import ExitStack

import concourse.mybir as mybir
from concourse.masks import make_identity

K, R, ITEMS, SLOTS = 512, 512, 2048, 512
FLOPS = 2 * 2 * K * R * SLOTS
EPS_INVERSE_SQUARE = 1.0e6

F32 = mybir.dt.float32
BF16 = mybir.dt.bfloat16
I32 = mybir.dt.int32
U32 = mybir.dt.uint32
U16 = mybir.dt.uint16
U8 = mybir.dt.uint8
FP8X4 = mybir.dt.float8_e4m3fn_x4
ACT = mybir.ActivationFunctionType
MULT = mybir.AluOpType.mult

P = 128
LANES = 4
QUADRANT = 32
ALIGN = 64

CHUNKS = (256, 256, 512, 512, 256, 256)
SCALAR_WEAVES = 2
STORE_AFTER = (2, 3, 4, 5)

TURN_BANKS, DEN_BANKS, NUM_BANKS = 2, 3, 3


def tile_attend_gnmf_pl_kernel(tc, fT, vT, H, wT, wU, fk, offs, out_0, out_1, out_2):
    nc = tc.nc
    with ExitStack() as ctx:
        keep = ctx.enter_context(tc.tile_pool(name="keep", bufs=1))
        ring = ctx.enter_context(tc.tile_pool(name="ring", bufs=2))
        psum = ctx.enter_context(tc.psum_pool(name="psum", bufs=1))

        def slot(shape, dtype, name, after=None):
            return keep.tile(shape, dtype, name=name, tag=after or name, align_bytes=ALIGN)

        def by_lane(rows):
            return rows.rearrange("(p t) c -> p t c", t=LANES)

        def load_lane(name, table, t):
            tile = slot([P, ITEMS], F32, f"{name}{t}")
            nc.sync.dma_start(tile[:], by_lane(table)[:, t, :])
            return tile

        h_rows = keep.tile([P, LANES, R], F32, name="h_rows")
        nc.sync.dma_start(h_rows[:], by_lane(H))
        offsets = keep.tile([P, SLOTS // 16], U16, name="offsets")
        nc.sync.dma_start(offsets[:], offs)
        fk_lanes = keep.tile([P, LANES], F32, name="fk_lanes")
        nc.sync.dma_start(fk_lanes[:], fk.rearrange("(p t) o -> p (t o)", t=LANES))
        w_table = [load_lane("w_table", wT, t) for t in range(LANES)]
        f_first = keep.tile([P, R], F32, name="f_first")
        nc.sync.dma_start(f_first[:], by_lane(fT)[:, 0, :])
        v_table = [load_lane("v_table", vT, t) for t in range(LANES)]
        u_table = [load_lane("u_table", wU, 0)]
        f_rest = keep.tile([P, LANES - 1, R], F32, name="f_rest")
        nc.sync.dma_start(f_rest[:], by_lane(fT)[:, 1:, :])
        u_table.extend(load_lane("u_table", wU, t) for t in range(1, LANES))

        identity = keep.tile([P, P], F32, name="identity")
        make_identity(nc, identity[:])

        eps_source = keep.tile([P, 1], F32, name="eps_source")
        nc.vector.memset(eps_source[:], EPS_INVERSE_SQUARE)
        eps = keep.tile([P, 1], F32, name="eps")
        nc.scalar.activation(eps[:], eps_source[:], ACT.Abs_reciprocal_sqrt)

        result = [keep.tile([P, ITEMS], F32, name=f"result{t}") for t in range(LANES)]
        for t in range(LANES):
            nc.vector.memset(result[t][:], 0.0)

        def turn(name, rows, woven):
            halves = keep.tile([P, 2, P, 2], BF16, name=name, align_bytes=ALIGN)
            nc.scalar.copy(halves[:], rows.rearrange("m (p h e) -> m h p e", h=2, e=2))
            words = halves[:].rearrange("m h p e -> m (h p e)").bitcast(F32)
            bank = psum.tile([P, 2, P], F32, name="turned", bufs=TURN_BANKS)
            for h in range(2):
                nc.tensor.transpose(bank[:, h, :], words[:, h * P : (h + 1) * P], identity[:])
            woven_words = woven.rearrange("p m t -> p (m t)").bitcast(F32).rearrange("p (m h) -> p m h", h=2)
            nc.scalar.copy(woven_words, bank[:].rearrange("p h m -> p m h"))

        def quantize(codes, scales, woven):
            nc.vector.quantize_mx(out=codes.bitcast(FP8X4), scales=scales, in_=woven.rearrange("p c t -> p (c t)"))

        def gather_and_quantize(name, table):
            woven = slot([P, SLOTS, LANES], BF16, f"{name}_woven")
            for t in range(LANES):
                nc.vector.tensor_copy(woven[:, :, t], table[t][:].indirect(offsets[:]))
            codes = slot([P, SLOTS], U32, f"{name}_codes")
            scales = slot([P, SLOTS], U8, f"{name}_scales")
            quantize(codes[:], scales[:], woven[:])
            return codes[:], scales[:]

        def quantize_f(t, rows):
            woven = slot([P, P, LANES], BF16, f"f_woven{t}")
            turn(f"f_halves{t}", rows, woven[:])
            codes = slot([P, P], U32, f"f_codes{t}")
            scales = slot([P, P], U8, f"f_scales{t}")
            quantize(codes[:], scales[:], woven[:])
            return codes[:], scales[:]

        def product(name, banks, stationary, moving):
            bank = psum.tile([P, SLOTS], F32, name=name, bufs=banks)
            nc.tensor.matmul_mx(
                out=bank[:],
                lhsT=stationary[0].bitcast(FP8X4),
                lhsT_scale=stationary[1],
                rhs=moving[0].bitcast(FP8X4),
                rhs_scale=moving[1],
                start=True,
                stop=True,
            )
            return bank

        h_woven = slot([P, K, LANES], BF16, "h_woven")
        for t in range(LANES):
            turn(f"h_halves{t}", h_rows[:, t, :], h_woven[:, t * P : (t + 1) * P, :])
        h_codes = slot([P, K], U32, "h_codes")
        h_scales = slot([P, K], U8, "h_scales")
        quantize(h_codes[:], h_scales[:], h_woven[:])
        w_mx = gather_and_quantize("w", w_table)
        f_first_mx = quantize_f(0, f_first[:])

        inverse = []
        for t in range(LANES):
            rows = slice(t * P, (t + 1) * P)
            den = product("den", DEN_BANKS, (h_codes[:, rows], h_scales[:, rows]), w_mx)
            root = ring.tile([P, SLOTS], F32, name="root")
            nc.scalar.activation(root[:], den[:], ACT.Abs_reciprocal_sqrt, bias=eps[:])
            sign = ring.tile([P, SLOTS], F32, name="sign")
            nc.scalar.activation(sign[:], den[:], ACT.Sign, bias=eps[:])
            size = ring.tile([P, SLOTS], F32, name="size")
            nc.scalar.activation(size[:], root[:], ACT.Square)
            signed = keep.tile([P, SLOTS], F32, name=f"inverse{t}")
            nc.gpsimd.tensor_tensor(signed[:], size[:], sign[:], MULT)
            inverse.append(signed)

        v_mx = gather_and_quantize("v", v_table)

        def numerator(t, f_mx):
            num = product("num", NUM_BANKS, f_mx, v_mx)
            scaled = keep.tile([P, SLOTS], F32, name=f"scaled{t}")
            nc.scalar.activation(scaled[:], num[:], ACT.Copy, scale=fk_lanes[:, t : t + 1])
            return scaled

        def update(t, scaled, after=None):
            ratio = slot([P, SLOTS], F32, f"ratio{t}", after)
            nc.vector.tensor_tensor(ratio[:], u_table[t][:].indirect(offsets[:]), inverse[t][:], MULT)
            nc.vector.tensor_tensor(result[t][:].indirect(offsets[:]), ratio[:], scaled[:], MULT)
            nc.sync.dma_start(by_lane(out_0)[:, t, :], result[t][:])

        update(0, numerator(0, f_first_mx))
        later = [numerator(t, quantize_f(t, f_rest[:, t - 1, :])) for t in range(1, LANES)]
        update(1, later[0], after=f"f_woven{LANES - 1}")
        for t in range(2, LANES):
            update(t, later[t - 1])

        starts = [sum(CHUNKS[:c]) for c in range(len(CHUNKS))]
        pairs_after = ("f_scales2", "v_codes", "f_codes2", "f_codes3", "v_scales", "f_scales3")
        pairs = [slot([P, 2, width, 2], BF16, f"pairs{c}", pairs_after[c]) for c, width in enumerate(CHUNKS)]
        for t in range(LANES):
            for c, width in enumerate(CHUNKS):
                nc.scalar.copy(pairs[c][:, t // 2, :, t % 2], result[t][:, starts[c] : starts[c] + width])

        y_scales = slot([P, ITEMS], U8, "y_scales")
        words_out = out_1.rearrange("a p c t -> p (a c t)").bitcast(I32)
        stores = []
        for c in STORE_AFTER:
            first = stores[-1][1] if stores else 0
            end = starts[c] + CHUNKS[c]
            stores.append((first, end, slot([P, end - first], U32, f"y_codes{c}")))

        woven_after = ("w_table0", "w_table1", "w_table2", "w_table3", "v_table0", "u_table1")

        def weave(c):
            woven = slot([P, CHUNKS[c], LANES], BF16, f"y_woven{c}", woven_after[c])
            on_scalar = c >= len(CHUNKS) - SCALAR_WEAVES
            word = U32 if on_scalar else I32
            src = pairs[c][:].rearrange("p h c e -> p (h c e)").bitcast(word).rearrange("p (h c) -> p c h", h=2)
            dst = woven[:].rearrange("p c t -> p (c t)").bitcast(word).rearrange("p (c h) -> p c h", h=2)
            if on_scalar:
                nc.scalar.copy(dst, src)
            else:
                nc.vector.tensor_copy(dst, src)
            return woven

        def quantize_chunk(c, woven):
            start, stop = starts[c], starts[c] + CHUNKS[c]
            first, end, codes = [store for store in stores if store[1] >= stop][0]
            quantize(codes[:, start - first : stop - first], y_scales[:, start:stop], woven[:])
            if stop == end:
                nc.sync.dma_start(words_out[:, first:end], codes[:].bitcast(I32))

        y_woven = [weave(0)]
        for c in range(1, len(CHUNKS)):
            y_woven.append(weave(c))
            quantize_chunk(c - 1, y_woven[c - 1])
        quantize_chunk(len(CHUNKS) - 1, y_woven[-1])

        scales_out = out_2.rearrange("a b c -> (a b) c").bitcast(I32)
        for q in range(P // QUADRANT):
            queue = nc.scalar if q < 2 else nc.sync
            queue.dma_start(scales_out[4 * q : 4 * q + 4, :], y_scales[QUADRANT * q : QUADRANT * q + 4, :].bitcast(I32))
